import numpy as np
import ml_dtypes


def mxq(x, axis, fmt="e4m3"):
    dtype, down = {"e4m3": (ml_dtypes.float8_e4m3fn, 7), "e5m2": (ml_dtypes.float8_e5m2, 14)}[fmt]
    v = np.moveaxis(np.asarray(x, np.float32).astype(ml_dtypes.bfloat16).astype(np.float64), axis, -1)
    blocks = v.reshape(v.shape[:-1] + (-1, 32))
    amax = np.abs(blocks).max(-1, keepdims=True)
    byte = np.maximum(np.where(amax > 0, np.frexp(amax)[1] - 1 + 127, 0) - down, 1)
    scale = np.exp2(byte - 127.0)
    codes = (blocks / scale).astype(np.float32).astype(dtype).astype(np.float64)
    return np.moveaxis((codes * scale).reshape(v.shape), -1, axis)


WIDE = False


def mx_kscale(k):
    if not WIDE:
        return np.ones(k)
    levels = np.array([10, -10, 5, -5, 0])
    if k % 512:
        return np.exp2(np.random.permutation(np.resize(levels, k // 32))).repeat(32)
    a = np.empty((k // 512, 16))
    for p in range(k // 512):
        a[p, :8] = np.random.permutation(np.resize(levels, 8))
        for g in range(8):
            far = levels[np.abs(levels - a[p, g]) >= 10]
            a[p, g + 8] = far[np.random.randint(len(far))]
    return np.exp2(a.ravel()).repeat(32)


def f64(x):
    return np.asarray(x).astype(np.float64)


def striped(idx):
    return np.tile(idx.reshape(-1, 16).T, (8, 1)).astype(np.uint16)


def unstriped(offs):
    return offs[:16].T.reshape(-1).astype(np.int64)


def striped8(idx):
    return np.concatenate([x.reshape(-1, 16).T for x in idx]).astype(np.uint16)


def runs(offs, k):
    lists = np.stack([offs[16 * r : 16 * r + 16].T.reshape(-1) for r in range(8)]).astype(np.int64)
    return lists[np.arange(k) % 512 // 64]


def pack_weight(w):
    k, n = w.shape
    w = f64(np.asarray(w, np.float32).astype(ml_dtypes.bfloat16)).reshape(k // 32, 32, n)
    amax = np.abs(w).max(1)
    byte = np.clip(np.where(amax > 0, np.frexp(amax)[1] - 1 + 127 - 7, 1), 1, 254)
    scaled = (w * np.exp2(127.0 - byte)[:, None, :]).reshape(k, n).astype(np.float32)
    words = np.ascontiguousarray(scaled.reshape(k // 512, 128, 4, n).transpose(0, 1, 3, 2)).astype(ml_dtypes.float8_e4m3fn).view(np.uint8)
    return words, np.ascontiguousarray(byte.astype(np.uint8).reshape(k // 512, 16, n))


def unpack_weight(words, scales):
    g, p, n, _ = words.shape
    vals = np.ascontiguousarray(words).view(ml_dtypes.float8_e4m3fn).astype(np.float64) * np.repeat(np.exp2(scales.astype(np.float64) - 127.0), 8, axis=1)[..., None]
    return vals.transpose(0, 1, 3, 2).reshape(g * 512, n)


K, T, S, V, H, G, U = 512, 2048, 1024, 512, 512, 2048, 1024


def setup_inputs():
    n = np.random.standard_normal
    s = mx_kscale(K)[:, None]
    packed_xT = pack_weight(n((K, T)) * s)
    packed_dT = pack_weight(n((K, G)) / s)
    return {
        "x_words": packed_xT[0],
        "x_scales": packed_xT[1],
        "w1": (n((K, H)) / np.sqrt(K) / s).astype(np.float32),
        "gs": (np.random.uniform(0.5, 1.5, (K, 1)) * s).astype(np.float32),
        "d_words": packed_dT[0],
        "d_scales": packed_dT[1],
        "mem": n((H, U)).astype(np.float32),
        "offs": striped(np.random.permutation(T)[:S]),
        "n1": striped8(np.stack([np.random.permutation(S) for _ in range(8)])),
        "k1": striped8(np.random.randint(0, G, (8, H))),
        "n2": striped8(np.stack([np.random.permutation(U)[:V] for _ in range(8)])),
    }


def reference(x_words, x_scales, w1, gs, d_words, d_scales, mem, offs, n1, k1, n2):
    d_k1 = unpack_weight(d_words, d_scales)[np.arange(K)[:, None], runs(k1, K)]
    xq = unpack_weight(x_words, x_scales)[:, unstriped(offs)]
    y = mxq(f64(w1), 0, "e4m3").T @ xq
    ln = y[np.arange(H)[:, None], runs(n1, H)]
    z = f64(gs) * (ln.reshape(H, V, 2).max(axis=2))
    h = 0.0625 * ((d_k1.T @ mxq(z, 0, "e4m3")))
    nw = np.maximum(h, 0.5 * (f64(mem)[np.arange(H)[:, None], runs(n2, H)]))
    out = f64(mem).copy()
    out[np.arange(H)[:, None], runs(n2, H)] = nw
    return out

@@ -1,0 +1,169 @@
+from contextlib import ExitStack
+
+import concourse.mybir as mybir
+
+K, T, S, V, H, G, U = 512, 2048, 1024, 512, 512, 2048, 1024
+FLOPS = 2 * K * H * S + 2 * K * H * V
+
+F32 = mybir.dt.float32
+BF16 = mybir.dt.bfloat16
+I32 = mybir.dt.int32
+U32 = mybir.dt.uint32
+U16 = mybir.dt.uint16
+U8 = mybir.dt.uint8
+FP8X4 = mybir.dt.float8_e4m3fn_x4
+ALU = mybir.AluOpType
+COPY = mybir.ActivationFunctionType.Copy
+
+P = 128
+PACK = 4
+BANK = 512
+
+
+def tile_picked_densepoolpagex_none_p_kernel(
+    tc, x_words, x_scales, w1, gs, d_words, d_scales, mem, offs, n1, k1, n2, out
+):
+    nc = tc.nc
+    with ExitStack() as ctx:
+        keep = ctx.enter_context(tc.tile_pool(name="keep", bufs=1))
+        psum = ctx.enter_context(tc.psum_pool(name="psum", bufs=8))
+
+        offs_sb = keep.tile([P, S // 16], U16, name="offs_sb")
+        n1_sb = keep.tile([P, S // 16], U16, name="n1_sb")
+        k1_sb = keep.tile([P, H // 16], U16, name="k1_sb")
+        n2_sb = keep.tile([P, V // 16], U16, name="n2_sb")
+
+        x_word_table = keep.tile([P, T], U32, name="x_word_table", tag="slot_c", align_bytes=64)
+        x_byte_table = keep.tile([P, T], U8, name="x_byte_table", tag="slot_d")
+        d_byte_table = keep.tile([P, G], U8, name="d_byte_table")
+        d_plane = keep.tile([P, H], U8, name="d_plane", align_bytes=64)
+        x_plane = keep.tile([P, S], U8, name="x_plane", align_bytes=64)
+        w_raw = [keep.tile([P, PACK, H // 2], F32, name=f"w_raw{a}", tag=f"slot_w{a}", align_bytes=64) for a in range(2)]
+        gs_sb = keep.tile([P, PACK], F32, name="gs_sb")
+
+        nc.vector.memset(x_byte_table[:].bitcast(I32), 0)
+        nc.vector.memset(d_byte_table[:].bitcast(I32), 0)
+        nc.vector.memset(x_plane[:].bitcast(I32), 0)
+        nc.vector.memset(d_plane[:].bitcast(I32), 0)
+
+        nc.sync.dma_start(offs_sb[:], offs)
+        nc.sync.dma_start(k1_sb[:], k1)
+        nc.sync.dma_start(n1_sb[:], n1)
+        nc.sync.dma_start(n2_sb[:], n2)
+        nc.sync.dma_start(x_byte_table[0:P:8, :].bitcast(I32), x_scales[0].bitcast(I32))
+        nc.sync.dma_start(d_byte_table[0:P:8, :].bitcast(I32), d_scales[0].bitcast(I32))
+        nc.sync.dma_start(x_word_table[:].bitcast(I32), x_words[0].rearrange("p n r -> p (n r)").bitcast(I32))
+        w_rows = w1.rearrange("(p j) c -> p j c", j=PACK)
+        for a in range(2):
+            nc.sync.dma_start(w_raw[a][:], w_rows[:, :, a * (H // 2) : (a + 1) * (H // 2)])
+        nc.sync.dma_start(gs_sb[:], gs.rearrange("(p t) o -> p (t o)", t=PACK))
+        mem_rows = mem.rearrange("(p t) u -> p t u", t=PACK)
+        out_rows = out.rearrange("(p t) u -> p t u", t=PACK)
+
+        x_bytes_picked = keep.tile([P, S], U8, name="x_bytes_picked")
+        x_codes = keep.tile([P, S], U32, name="x_codes", align_bytes=64)
+        nc.vector.tensor_copy(x_bytes_picked[:], x_byte_table[:].indirect(offs_sb[:]))
+        for j in range(4):
+            nc.sync.dma_start(x_plane[j:P:32, :].bitcast(I32), x_bytes_picked[8 * j : P : 32, :].bitcast(I32))
+        d_word_table = keep.tile([P, G], U32, name="d_word_table", tag="slot_d")
+        nc.sync.dma_start(d_word_table[:].bitcast(I32), d_words[0].rearrange("p n r -> p (n r)").bitcast(I32))
+        nc.vector.tensor_copy(x_codes[:], x_word_table[:].indirect(offs_sb[:]))
+
+        w_grouped = keep.tile([P, PACK, P, PACK], BF16, name="w_grouped", align_bytes=64, tag="slot_g")
+        for a in range(2):
+            nc.scalar.copy(
+                w_grouped[:, :, a * (P // 2) : (a + 1) * (P // 2), :].rearrange("p t m j -> p m t j"),
+                w_raw[a][:].rearrange("p j (m t) -> p m t j", t=PACK),
+            )
+        d_bytes_picked = keep.tile([P, H], U8, name="d_bytes_picked")
+        nc.vector.tensor_copy(d_bytes_picked[:], d_byte_table[:].indirect(k1_sb[:]))
+        w_codes = keep.tile([P, H], U32, name="w_codes", align_bytes=64)
+        w_plane = keep.tile([P, H], U8, name="w_plane", align_bytes=64)
+        nc.vector.quantize_mx(
+            out=w_codes[:].bitcast(FP8X4), scales=w_plane[:], in_=w_grouped[:].rearrange("p t m j -> p (t m j)")
+        )
+
+        page = [
+            keep.tile([P, U], F32, name=f"page{t}", tag=tag, align_bytes=64)
+            for t, tag in enumerate(("slot_c", "slot_w0", "slot_w1", "slot_g"))
+        ]
+        for t in range(PACK):
+            nc.sync.dma_start(page[t][:], mem_rows[:, t, :])
+
+        y = [keep.tile([P, S], F32, name=f"y{t}") for t in range(PACK)]
+        for t in range(PACK):
+            m_cols = slice(t * P, (t + 1) * P)
+            for a in range(S // BANK):
+                n_cols = slice(a * BANK, (a + 1) * BANK)
+                acc = psum.tile([P, BANK], F32, name="acc")
+                nc.tensor.matmul_mx(
+                    out=acc[:],
+                    lhsT=w_codes[:, m_cols].bitcast(FP8X4),
+                    lhsT_scale=w_plane[:, m_cols],
+                    rhs=x_codes[:, n_cols].bitcast(FP8X4),
+                    rhs_scale=x_plane[:, n_cols],
+                    start=True,
+                    stop=True,
+                )
+                nc.scalar.copy(y[t][:, n_cols], acc[:])
+
+        d_words_picked = keep.tile([P, H], U32, name="d_words_picked")
+        nc.vector.tensor_copy(d_words_picked[:], d_word_table[:].indirect(k1_sb[:]))
+        d_bytes_dealt = keep.tile([P, H], U8, name="d_bytes_dealt")
+        d_codes = keep.tile([P, H], U32, name="d_codes", align_bytes=64)
+        for dealt, picked in ((d_bytes_dealt, d_bytes_picked), (d_codes, d_words_picked)):
+            nc.vector.tensor_copy(
+                dealt[:].rearrange("p (t c i) -> p c t i", t=PACK, i=4),
+                picked[:].rearrange("p (c i t) -> p c t i", t=PACK, i=4),
+            )
+        for j in range(4):
+            nc.sync.dma_start(d_plane[j:P:32, :].bitcast(I32), d_bytes_dealt[8 * j : P : 32, :].bitcast(I32))
+
+        z_grouped = keep.tile([P, V, PACK], BF16, name="z_grouped", align_bytes=64)
+        for t in range(PACK):
+            if t < PACK - 1:
+                lined = keep.tile([P, S], F32, name=f"lined{t}")
+            else:
+                lined = keep.tile([P, 2 * S], F32, name="lined_last", tag="last")
+            for a in range(2):
+                nc.vector.tensor_copy(
+                    lined[:, a * 512 : (a + 1) * 512], y[t][:].indirect(n1_sb[:, a * 32 : (a + 1) * 32])
+                )
+            pooled = keep.tile([P, V], F32, name=f"pooled{t}")
+            nc.vector.tensor_tensor(pooled[:], lined[:, 0:S:2], lined[:, 1:S:2], ALU.max)
+            nc.scalar.activation(z_grouped[:, :, t], pooled[:], COPY, scale=gs_sb[:, t : t + 1])
+
+        old = keep.tile([P, PACK * V], F32, name="old", tag="last")
+        for t in range(2):
+            nc.vector.tensor_scalar(
+                old[:, t * V : (t + 1) * V], page[t][:].indirect(n2_sb[:]), 0.5, 0.0, ALU.mult, ALU.add
+            )
+        z_codes = keep.tile([P, V], U32, name="z_codes", align_bytes=64)
+        z_plane = keep.tile([P, V], U8, name="z_plane", align_bytes=64)
+        nc.vector.quantize_mx(
+            out=z_codes[:].bitcast(FP8X4), scales=z_plane[:], in_=z_grouped[:].rearrange("p v t -> p (v t)")
+        )
+        for t in range(2, PACK):
+            nc.vector.tensor_scalar(
+                old[:, t * V : (t + 1) * V], page[t][:].indirect(n2_sb[:]), 0.5, 0.0, ALU.mult, ALU.add
+            )
+
+        new = []
+        for t in range(PACK):
+            m_cols = slice(t * P, (t + 1) * P)
+            acc = psum.tile([P, BANK], F32, name="acc")
+            nc.tensor.matmul_mx(
+                out=acc[:],
+                lhsT=d_codes[:, m_cols].bitcast(FP8X4),
+                lhsT_scale=d_plane[:, m_cols],
+                rhs=z_codes[:].bitcast(FP8X4),
+                rhs_scale=z_plane[:],
+                start=True,
+                stop=True,
+            )
+            nw = keep.tile([P, V], F32, name=f"new{t}")
+            nc.vector.scalar_tensor_tensor(nw[:], acc[:], 0.0625, old[:, t * V : (t + 1) * V], ALU.mult, ALU.max)
+            new.append(nw)
+        for t in range(PACK):
+            nc.vector.tensor_copy(page[t][:].indirect(n2_sb[:]), new[t][:])
+            nc.sync.dma_start(out_rows[:, t, :], page[t][:])

@@ -1,6 +1,7 @@
 from contextlib import ExitStack
 
 import concourse.mybir as mybir
+from concourse.masks import make_identity
 
 K, T, S, V, H, G, U = 512, 2048, 1024, 512, 512, 2048, 1024
 FLOPS = 2 * K * H * S + 2 * K * H * V
@@ -14,6 +15,7 @@ U8 = mybir.dt.uint8
 FP8X4 = mybir.dt.float8_e4m3fn_x4
 ALU = mybir.AluOpType
 COPY = mybir.ActivationFunctionType.Copy
+RELU = mybir.ActivationFunctionType.Relu
 
 P = 128
 PACK = 4
@@ -34,7 +36,7 @@ def tile_picked_densepoolpagex_none_p_kernel(
         n2_sb = keep.tile([P, V // 16], U16, name="n2_sb")
 
         x_word_table = keep.tile([P, T], U32, name="x_word_table", tag="slot_c", align_bytes=64)
-        x_byte_table = keep.tile([P, T], U8, name="x_byte_table", tag="slot_d")
+        x_byte_table = keep.tile([P, T], U8, name="x_byte_table")
         d_byte_table = keep.tile([P, G], U8, name="d_byte_table")
         d_plane = keep.tile([P, H], U8, name="d_plane", align_bytes=64)
         x_plane = keep.tile([P, S], U8, name="x_plane", align_bytes=64)
@@ -47,55 +49,64 @@ def tile_picked_densepoolpagex_none_p_kernel(
         nc.vector.memset(d_plane[:].bitcast(I32), 0)
 
         nc.sync.dma_start(offs_sb[:], offs)
+        nc.sync.dma_start(x_byte_table[0:P:8, :].bitcast(I32), x_scales[0].bitcast(I32))
         nc.sync.dma_start(k1_sb[:], k1)
         nc.sync.dma_start(n1_sb[:], n1)
         nc.sync.dma_start(n2_sb[:], n2)
-        nc.sync.dma_start(x_byte_table[0:P:8, :].bitcast(I32), x_scales[0].bitcast(I32))
         nc.sync.dma_start(d_byte_table[0:P:8, :].bitcast(I32), d_scales[0].bitcast(I32))
         nc.sync.dma_start(x_word_table[:].bitcast(I32), x_words[0].rearrange("p n r -> p (n r)").bitcast(I32))
         w_rows = w1.rearrange("(p j) c -> p j c", j=PACK)
         for a in range(2):
             nc.sync.dma_start(w_raw[a][:], w_rows[:, :, a * (H // 2) : (a + 1) * (H // 2)])
+        d_word_table = keep.tile([P, G], U32, name="d_word_table")
+        nc.sync.dma_start(d_word_table[:].bitcast(I32), d_words[0].rearrange("p n r -> p (n r)").bitcast(I32))
         nc.sync.dma_start(gs_sb[:], gs.rearrange("(p t) o -> p (t o)", t=PACK))
         mem_rows = mem.rearrange("(p t) u -> p t u", t=PACK)
         out_rows = out.rearrange("(p t) u -> p t u", t=PACK)
 
         x_bytes_picked = keep.tile([P, S], U8, name="x_bytes_picked")
-        x_codes = keep.tile([P, S], U32, name="x_codes", align_bytes=64)
+        w_grouped = keep.tile([P, PACK, P, PACK], BF16, name="w_grouped", align_bytes=64, tag="slot_q")
         nc.vector.tensor_copy(x_bytes_picked[:], x_byte_table[:].indirect(offs_sb[:]))
-        for j in range(4):
-            nc.sync.dma_start(x_plane[j:P:32, :].bitcast(I32), x_bytes_picked[8 * j : P : 32, :].bitcast(I32))
-        d_word_table = keep.tile([P, G], U32, name="d_word_table", tag="slot_d")
-        nc.sync.dma_start(d_word_table[:].bitcast(I32), d_words[0].rearrange("p n r -> p (n r)").bitcast(I32))
-        nc.vector.tensor_copy(x_codes[:], x_word_table[:].indirect(offs_sb[:]))
+        for q in range(0, P, 32):
+            nc.sync.dma_start(x_plane[q : q + 4, :].bitcast(I32), x_bytes_picked[q : q + 32 : 8, :].bitcast(I32))
 
-        w_grouped = keep.tile([P, PACK, P, PACK], BF16, name="w_grouped", align_bytes=64, tag="slot_g")
-        for a in range(2):
-            nc.scalar.copy(
-                w_grouped[:, :, a * (P // 2) : (a + 1) * (P // 2), :].rearrange("p t m j -> p m t j"),
-                w_raw[a][:].rearrange("p j (m t) -> p m t j", t=PACK),
-            )
         d_bytes_picked = keep.tile([P, H], U8, name="d_bytes_picked")
         nc.vector.tensor_copy(d_bytes_picked[:], d_byte_table[:].indirect(k1_sb[:]))
+        x_codes = keep.tile([P, S], U32, name="x_codes", align_bytes=64, tag="slot_g")
+        nc.vector.tensor_copy(x_codes[:], x_word_table[:].indirect(offs_sb[:]))
+
+        def group_w1(copy, a, tiles):
+            copy(
+                w_grouped[:, tiles, a * (P // 2) : (a + 1) * (P // 2), :].rearrange("p t m j -> p m t j"),
+                w_raw[a][:].rearrange("p j (m t) -> p m t j", t=PACK)[:, :, tiles, :],
+            )
+
+        group_w1(nc.scalar.copy, 0, slice(0, PACK))
+        group_w1(nc.scalar.copy, 1, slice(1, PACK))
+        group_w1(nc.vector.tensor_copy, 1, slice(0, 1))
         w_codes = keep.tile([P, H], U32, name="w_codes", align_bytes=64)
         w_plane = keep.tile([P, H], U8, name="w_plane", align_bytes=64)
-        nc.vector.quantize_mx(
-            out=w_codes[:].bitcast(FP8X4), scales=w_plane[:], in_=w_grouped[:].rearrange("p t m j -> p (t m j)")
-        )
+        for tiles in (slice(0, 1), slice(1, 2), slice(2, 4)):
+            cols = slice(tiles.start * P, tiles.stop * P)
+            nc.vector.quantize_mx(
+                out=w_codes[:, cols].bitcast(FP8X4),
+                scales=w_plane[:, cols],
+                in_=w_grouped[:, tiles, :, :].rearrange("p t m j -> p (t m j)"),
+            )
 
         page = [
             keep.tile([P, U], F32, name=f"page{t}", tag=tag, align_bytes=64)
-            for t, tag in enumerate(("slot_c", "slot_w0", "slot_w1", "slot_g"))
+            for t, tag in enumerate(("slot_w0", "slot_c", "slot_w1", "slot_q"))
         ]
         for t in range(PACK):
             nc.sync.dma_start(page[t][:], mem_rows[:, t, :])
 
         y = [keep.tile([P, S], F32, name=f"y{t}") for t in range(PACK)]
         for t in range(PACK):
-            m_cols = slice(t * P, (t + 1) * P)
             for a in range(S // BANK):
-                n_cols = slice(a * BANK, (a + 1) * BANK)
+                m_cols = slice(t * P, (t + 1) * P)
                 acc = psum.tile([P, BANK], F32, name="acc")
+                n_cols = slice(a * BANK, (a + 1) * BANK)
                 nc.tensor.matmul_mx(
                     out=acc[:],
                     lhsT=w_codes[:, m_cols].bitcast(FP8X4),
@@ -105,65 +116,127 @@ def tile_picked_densepoolpagex_none_p_kernel(
                     start=True,
                     stop=True,
                 )
-                nc.scalar.copy(y[t][:, n_cols], acc[:])
+                nc.scalar.copy(y[t][:, a * BANK : (a + 1) * BANK], acc[:])
 
-        d_words_picked = keep.tile([P, H], U32, name="d_words_picked")
+        d_words_picked = keep.tile([P, H], U32, name="d_words_picked", align_bytes=64)
         nc.vector.tensor_copy(d_words_picked[:], d_word_table[:].indirect(k1_sb[:]))
-        d_bytes_dealt = keep.tile([P, H], U8, name="d_bytes_dealt")
-        d_codes = keep.tile([P, H], U32, name="d_codes", align_bytes=64)
-        for dealt, picked in ((d_bytes_dealt, d_bytes_picked), (d_codes, d_words_picked)):
-            nc.vector.tensor_copy(
-                dealt[:].rearrange("p (t c i) -> p c t i", t=PACK, i=4),
-                picked[:].rearrange("p (c i t) -> p c t i", t=PACK, i=4),
-            )
-        for j in range(4):
-            nc.sync.dma_start(d_plane[j:P:32, :].bitcast(I32), d_bytes_dealt[8 * j : P : 32, :].bitcast(I32))
+        for q in range(0, P, 32):
+            nc.sync.dma_start(d_plane[q : q + 4, :].bitcast(I32), d_bytes_picked[q : q + 32 : 8, :].bitcast(I32))
 
-        z_grouped = keep.tile([P, V, PACK], BF16, name="z_grouped", align_bytes=64)
-        for t in range(PACK):
-            if t < PACK - 1:
-                lined = keep.tile([P, S], F32, name=f"lined{t}")
-            else:
-                lined = keep.tile([P, 2 * S], F32, name="lined_last", tag="last")
-            for a in range(2):
-                nc.vector.tensor_copy(
-                    lined[:, a * 512 : (a + 1) * 512], y[t][:].indirect(n1_sb[:, a * 32 : (a + 1) * 32])
+        ident = keep.tile([P, P], F32, name="ident")
+        make_identity(nc, ident[:])
+
+        HV = V // 2
+
+        def line_up(a, lined, z_grouped, groups):
+            for tiles in groups:
+                for t in tiles:
+                    nc.vector.tensor_copy(lined[:, t, :], y[t][:].indirect(n1_sb[:, a * 32 : (a + 1) * 32]))
+                pairs = lined[:, tiles.start : tiles.stop, :].rearrange("p i (v two) -> p (i v) two", two=2)
+                pooled = keep.tile([P, len(tiles) * HV], F32, name=f"pooled{a}{tiles.start}")
+                nc.vector.tensor_tensor(pooled[:], pairs[:, :, 0], pairs[:, :, 1], ALU.max)
+                for i, t in enumerate(tiles):
+                    nc.scalar.activation(
+                        z_grouped[:, :, t], pooled[:, i * HV : (i + 1) * HV], COPY, scale=gs_sb[:, t : t + 1]
+                    )
+
+        def fetch_old(a, old):
+            for t in range(PACK):
+                nc.vector.tensor_scalar(
+                    old[:, t, :], page[t][:].indirect(n2_sb[:, a * 16 : (a + 1) * 16]), 0.5, 0.0, ALU.mult, ALU.add
                 )
-            pooled = keep.tile([P, V], F32, name=f"pooled{t}")
-            nc.vector.tensor_tensor(pooled[:], lined[:, 0:S:2], lined[:, 1:S:2], ALU.max)
-            nc.scalar.activation(z_grouped[:, :, t], pooled[:], COPY, scale=gs_sb[:, t : t + 1])
 
-        old = keep.tile([P, PACK * V], F32, name="old", tag="last")
-        for t in range(2):
-            nc.vector.tensor_scalar(
-                old[:, t * V : (t + 1) * V], page[t][:].indirect(n2_sb[:]), 0.5, 0.0, ALU.mult, ALU.add
+        def quantise(a, z_grouped):
+            z_codes = keep.tile([P, HV], U32, name=f"z_codes{a}", align_bytes=64)
+            z_plane = keep.tile([P, HV], U8, name=f"z_plane{a}", align_bytes=64)
+            nc.vector.quantize_mx(
+                out=z_codes[:].bitcast(FP8X4), scales=z_plane[:], in_=z_grouped[:].rearrange("p v t -> p (v t)")
             )
-        z_codes = keep.tile([P, V], U32, name="z_codes", align_bytes=64)
-        z_plane = keep.tile([P, V], U8, name="z_plane", align_bytes=64)
-        nc.vector.quantize_mx(
-            out=z_codes[:].bitcast(FP8X4), scales=z_plane[:], in_=z_grouped[:].rearrange("p v t -> p (v t)")
-        )
-        for t in range(2, PACK):
-            nc.vector.tensor_scalar(
-                old[:, t * V : (t + 1) * V], page[t][:].indirect(n2_sb[:]), 0.5, 0.0, ALU.mult, ALU.add
-            )
+            return z_codes, z_plane
 
-        new = []
-        for t in range(PACK):
-            m_cols = slice(t * P, (t + 1) * P)
-            acc = psum.tile([P, BANK], F32, name="acc")
-            nc.tensor.matmul_mx(
-                out=acc[:],
-                lhsT=d_codes[:, m_cols].bitcast(FP8X4),
-                lhsT_scale=d_plane[:, m_cols],
-                rhs=z_codes[:].bitcast(FP8X4),
-                rhs_scale=z_plane[:],
-                start=True,
-                stop=True,
-            )
-            nw = keep.tile([P, V], F32, name=f"new{t}")
-            nc.vector.scalar_tensor_tensor(nw[:], acc[:], 0.0625, old[:, t * V : (t + 1) * V], ALU.mult, ALU.max)
-            new.append(nw)
-        for t in range(PACK):
-            nc.vector.tensor_copy(page[t][:].indirect(n2_sb[:]), new[t][:])
-            nc.sync.dma_start(out_rows[:, t, :], page[t][:])
+        def turn_old(a, old, tags):
+            old_t = []
+            for u in range(2):
+                acc = psum.tile([P, 2, 2, P], F32, name="acc")
+                for i in range(2):
+                    for b in range(2):
+                        nc.tensor.transpose(acc[:, i, b, :], old[:, 2 * u + i, b * P : (b + 1) * P], ident[:])
+                turned = keep.tile([P, 2, 2, P], F32, name=f"old_t{a}{u}", tag=tags[u], align_bytes=64)
+                nc.scalar.copy(turned[:], acc[:])
+                old_t.append(turned)
+            return old_t
+
+        def second_product(a, z_codes, z_plane):
+            neg_h_t = []
+            for b in range(2):
+                cols = slice(b * P, (b + 1) * P)
+                acc = psum.tile([P, BANK], F32, name="acc")
+                nc.tensor.matmul_mx(
+                    out=acc[:],
+                    lhsT=z_codes[:, cols].bitcast(FP8X4),
+                    lhsT_scale=z_plane[:, cols],
+                    rhs=d_words_picked[:].bitcast(FP8X4),
+                    rhs_scale=d_plane[:],
+                    start=True,
+                    stop=True,
+                )
+                dealt = keep.tile([P, PACK, P], F32, name=f"neg_h_t{a}{b}")
+                nc.scalar.activation(dealt[:], acc[:].rearrange("p (m t) -> p t m", t=PACK), COPY, scale=-0.0625)
+                neg_h_t.append(dealt)
+            return neg_h_t
+
+        def turn_back(u, neg_h_t, old_t):
+            neg_h = psum.tile([P, 2, HV], F32, name="acc")
+            gap = psum.tile([P, 2, HV], F32, name="acc")
+            for i in range(2):
+                for b in range(2):
+                    nc.tensor.transpose(neg_h[:, i, b * P : (b + 1) * P], neg_h_t[b][:, 2 * u + i, :], ident[:])
+            for i in range(2):
+                for b in range(2):
+                    cols = slice(b * P, (b + 1) * P)
+                    nc.tensor.matmul(
+                        gap[:, i, cols], old_t[u][:, i, b, :], ident[:], start=True, stop=False, is_transpose=True
+                    )
+                    nc.tensor.matmul(
+                        gap[:, i, cols], neg_h_t[b][:, 2 * u + i, :], ident[:], start=False, stop=True, is_transpose=True
+                    )
+            return neg_h, gap
+
+        def leave_banks(a, u, banks):
+            neg_h, gap = banks
+            h = keep.tile([P, 2, HV], F32, name=f"h{a}{u}")
+            nc.scalar.activation(h[:], neg_h[:], COPY, scale=-1.0)
+            lift = keep.tile([P, 2, HV], F32, name=f"lift{a}{u}")
+            nc.scalar.activation(lift[:], gap[:], RELU)
+            return [(h[:, i, :], lift[:, i, :]) for i in range(2)]
+
+        def scatter(a, t, terms):
+            nc.vector.tensor_tensor(page[t][:].indirect(n2_sb[:, a * 16 : (a + 1) * 16]), *terms, ALU.add)
+
+        z0 = keep.tile([P, HV, PACK], BF16, name="z0", align_bytes=64, tag="slot_g")
+        lined0 = keep.tile([P, PACK, 2 * HV], F32, name="lined0", tag="slot_l0")
+        line_up(0, lined0, z0, (range(0, 2), range(2, 4)))
+        old0 = keep.tile([P, PACK, HV], F32, name="old0", tag="slot_l0")
+        fetch_old(0, old0)
+        q0 = quantise(0, z0)
+        old_t0 = turn_old(0, old0, ("slot_z", "slot_o1"))
+        neg_h_t0 = second_product(0, *q0)
+        banks0 = [turn_back(u, neg_h_t0, old_t0) for u in range(2)]
+        terms0 = leave_banks(0, 0, banks0[0])
+        z1 = keep.tile([P, HV, PACK], BF16, name="z1", align_bytes=64, tag="slot_z")
+        lined1 = keep.tile([P, PACK, 2 * HV], F32, name="lined1", align_bytes=64, tag="slot_g")
+        line_up(1, lined1, z1, (range(0, 2), range(2, 3), range(3, 4)))
+        scatter(0, 0, terms0[0])
+        terms0 = terms0 + leave_banks(0, 1, banks0[1])
+        q1 = quantise(1, z1)
+        late = keep.tile([P, PACK, HV], F32, name="late", align_bytes=64, tag="slot_z")
+        fetch_old(1, late)
+        neg_h_t1 = second_product(1, *q1)
+        for t in range(1, PACK):
+            scatter(0, t, terms0[t])
+        old_t1 = turn_old(1, late, ("slot_o2", "slot_o3"))
+        for u in range(2):
+            terms = leave_banks(1, u, turn_back(u, neg_h_t1, old_t1))
+            for i in range(2):
+                scatter(1, 2 * u + i, terms[i])
+                nc.sync.dma_start(out_rows[:, 2 * u + i, :], page[2 * u + i][:])

@@ -140,11 +140,15 @@ def tile_picked_densepoolpagex_none_p_kernel(
                         z_grouped[:, :, t], pooled[:, i * HV : (i + 1) * HV], COPY, scale=gs_sb[:, t : t + 1]
                     )
 
-        def fetch_old(a, old):
-            for t in range(PACK):
+        old_first = keep.tile([P, V], F32, name="old_first")
+        nc.vector.tensor_scalar(old_first[:], page[0][:].indirect(n2_sb[:]), 0.5, 0.0, ALU.mult, ALU.add)
+
+        def fetch_old(a, rest):
+            for t in range(1, PACK):
                 nc.vector.tensor_scalar(
-                    old[:, t, :], page[t][:].indirect(n2_sb[:, a * 16 : (a + 1) * 16]), 0.5, 0.0, ALU.mult, ALU.add
+                    rest[:, t - 1, :], page[t][:].indirect(n2_sb[:, a * 16 : (a + 1) * 16]), 0.5, 0.0, ALU.mult, ALU.add
                 )
+            return [old_first[:, a * HV : (a + 1) * HV]] + [rest[:, i, :] for i in range(PACK - 1)]
 
         def quantise(a, z_grouped):
             z_codes = keep.tile([P, HV], U32, name=f"z_codes{a}", align_bytes=64)
@@ -160,7 +164,7 @@ def tile_picked_densepoolpagex_none_p_kernel(
                 acc = psum.tile([P, 2, 2, P], F32, name="acc")
                 for i in range(2):
                     for b in range(2):
-                        nc.tensor.transpose(acc[:, i, b, :], old[:, 2 * u + i, b * P : (b + 1) * P], ident[:])
+                        nc.tensor.transpose(acc[:, i, b, :], old[2 * u + i][:, b * P : (b + 1) * P], ident[:])
                 turned = keep.tile([P, 2, 2, P], F32, name=f"old_t{a}{u}", tag=tags[u], align_bytes=64)
                 nc.scalar.copy(turned[:], acc[:])
                 old_t.append(turned)
@@ -216,8 +220,8 @@ def tile_picked_densepoolpagex_none_p_kernel(
         z0 = keep.tile([P, HV, PACK], BF16, name="z0", align_bytes=64, tag="slot_g")
         lined0 = keep.tile([P, PACK, 2 * HV], F32, name="lined0", tag="slot_l0")
         line_up(0, lined0, z0, (range(0, 2), range(2, 4)))
-        old0 = keep.tile([P, PACK, HV], F32, name="old0", tag="slot_l0")
-        fetch_old(0, old0)
+        rest0 = keep.tile([P, PACK - 1, HV], F32, name="rest0", tag="slot_l0")
+        old0 = fetch_old(0, rest0)
         q0 = quantise(0, z0)
         old_t0 = turn_old(0, old0, ("slot_z", "slot_o1"))
         neg_h_t0 = second_product(0, *q0)
@@ -229,12 +233,12 @@ def tile_picked_densepoolpagex_none_p_kernel(
         scatter(0, 0, terms0[0])
         terms0 = terms0 + leave_banks(0, 1, banks0[1])
         q1 = quantise(1, z1)
-        late = keep.tile([P, PACK, HV], F32, name="late", align_bytes=64, tag="slot_z")
-        fetch_old(1, late)
+        rest1 = keep.tile([P, PACK - 1, HV], F32, name="rest1", align_bytes=64, tag="slot_z")
+        old1 = fetch_old(1, rest1)
         neg_h_t1 = second_product(1, *q1)
         for t in range(1, PACK):
             scatter(0, t, terms0[t])
-        old_t1 = turn_old(1, late, ("slot_o2", "slot_o3"))
+        old_t1 = turn_old(1, old1, ("slot_o2", "slot_o3"))
         for u in range(2):
             terms = leave_banks(1, u, turn_back(u, neg_h_t1, old_t1))
             for i in range(2):

from contextlib import ExitStack

import concourse.mybir as mybir
from concourse.masks import make_identity

K, T, S, V, H, G, U = 512, 2048, 1024, 512, 512, 2048, 1024
FLOPS = 2 * K * H * S + 2 * K * H * V

F32 = mybir.dt.float32
BF16 = mybir.dt.bfloat16
I32 = mybir.dt.int32
U32 = mybir.dt.uint32
U16 = mybir.dt.uint16
U8 = mybir.dt.uint8
FP8X4 = mybir.dt.float8_e4m3fn_x4
ALU = mybir.AluOpType
COPY = mybir.ActivationFunctionType.Copy
RELU = mybir.ActivationFunctionType.Relu

P = 128
PACK = 4
BANK = 512


def tile_picked_densepoolpagex_none_p_kernel(
    tc, x_words, x_scales, w1, gs, d_words, d_scales, mem, offs, n1, k1, n2, out
):
    nc = tc.nc
    with ExitStack() as ctx:
        keep = ctx.enter_context(tc.tile_pool(name="keep", bufs=1))
        psum = ctx.enter_context(tc.psum_pool(name="psum", bufs=8))

        offs_sb = keep.tile([P, S // 16], U16, name="offs_sb")
        n1_sb = keep.tile([P, S // 16], U16, name="n1_sb")
        k1_sb = keep.tile([P, H // 16], U16, name="k1_sb")
        n2_sb = keep.tile([P, V // 16], U16, name="n2_sb")

        x_word_table = keep.tile([P, T], U32, name="x_word_table", tag="slot_c", align_bytes=64)
        x_byte_table = keep.tile([P, T], U8, name="x_byte_table")
        d_byte_table = keep.tile([P, G], U8, name="d_byte_table")
        d_plane = keep.tile([P, H], U8, name="d_plane", align_bytes=64)
        x_plane = keep.tile([P, S], U8, name="x_plane", align_bytes=64)
        w_raw = [keep.tile([P, PACK, H // 2], F32, name=f"w_raw{a}", tag=f"slot_w{a}", align_bytes=64) for a in range(2)]
        gs_sb = keep.tile([P, PACK], F32, name="gs_sb")

        nc.vector.memset(x_byte_table[:].bitcast(I32), 0)
        nc.vector.memset(d_byte_table[:].bitcast(I32), 0)
        nc.vector.memset(x_plane[:].bitcast(I32), 0)
        nc.vector.memset(d_plane[:].bitcast(I32), 0)

        nc.sync.dma_start(offs_sb[:], offs)
        nc.sync.dma_start(x_byte_table[0:P:8, :].bitcast(I32), x_scales[0].bitcast(I32))
        nc.sync.dma_start(k1_sb[:], k1)
        nc.sync.dma_start(n1_sb[:], n1)
        nc.sync.dma_start(n2_sb[:], n2)
        nc.sync.dma_start(d_byte_table[0:P:8, :].bitcast(I32), d_scales[0].bitcast(I32))
        nc.sync.dma_start(x_word_table[:].bitcast(I32), x_words[0].rearrange("p n r -> p (n r)").bitcast(I32))
        w_rows = w1.rearrange("(p j) c -> p j c", j=PACK)
        for a in range(2):
            nc.sync.dma_start(w_raw[a][:], w_rows[:, :, a * (H // 2) : (a + 1) * (H // 2)])
        d_word_table = keep.tile([P, G], U32, name="d_word_table")
        nc.sync.dma_start(d_word_table[:].bitcast(I32), d_words[0].rearrange("p n r -> p (n r)").bitcast(I32))
        nc.sync.dma_start(gs_sb[:], gs.rearrange("(p t) o -> p (t o)", t=PACK))
        mem_rows = mem.rearrange("(p t) u -> p t u", t=PACK)
        out_rows = out.rearrange("(p t) u -> p t u", t=PACK)

        x_bytes_picked = keep.tile([P, S], U8, name="x_bytes_picked")
        w_grouped = keep.tile([P, PACK, P, PACK], BF16, name="w_grouped", align_bytes=64, tag="slot_q")
        nc.vector.tensor_copy(x_bytes_picked[:], x_byte_table[:].indirect(offs_sb[:]))
        for q in range(0, P, 32):
            nc.sync.dma_start(x_plane[q : q + 4, :].bitcast(I32), x_bytes_picked[q : q + 32 : 8, :].bitcast(I32))

        d_bytes_picked = keep.tile([P, H], U8, name="d_bytes_picked")
        nc.vector.tensor_copy(d_bytes_picked[:], d_byte_table[:].indirect(k1_sb[:]))
        x_codes = keep.tile([P, S], U32, name="x_codes", align_bytes=64, tag="slot_g")
        nc.vector.tensor_copy(x_codes[:], x_word_table[:].indirect(offs_sb[:]))

        def group_w1(copy, a, tiles):
            copy(
                w_grouped[:, tiles, a * (P // 2) : (a + 1) * (P // 2), :].rearrange("p t m j -> p m t j"),
                w_raw[a][:].rearrange("p j (m t) -> p m t j", t=PACK)[:, :, tiles, :],
            )

        group_w1(nc.scalar.copy, 0, slice(0, PACK))
        group_w1(nc.scalar.copy, 1, slice(1, PACK))
        group_w1(nc.vector.tensor_copy, 1, slice(0, 1))
        w_codes = keep.tile([P, H], U32, name="w_codes", align_bytes=64)
        w_plane = keep.tile([P, H], U8, name="w_plane", align_bytes=64)
        for tiles in (slice(0, 1), slice(1, 2), slice(2, 4)):
            cols = slice(tiles.start * P, tiles.stop * P)
            nc.vector.quantize_mx(
                out=w_codes[:, cols].bitcast(FP8X4),
                scales=w_plane[:, cols],
                in_=w_grouped[:, tiles, :, :].rearrange("p t m j -> p (t m j)"),
            )

        page = [
            keep.tile([P, U], F32, name=f"page{t}", tag=tag, align_bytes=64)
            for t, tag in enumerate(("slot_w0", "slot_c", "slot_w1", "slot_q"))
        ]
        for t in range(PACK):
            nc.sync.dma_start(page[t][:], mem_rows[:, t, :])

        y = [keep.tile([P, S], F32, name=f"y{t}") for t in range(PACK)]
        for t in range(PACK):
            for a in range(S // BANK):
                m_cols = slice(t * P, (t + 1) * P)
                acc = psum.tile([P, BANK], F32, name="acc")
                n_cols = slice(a * BANK, (a + 1) * BANK)
                nc.tensor.matmul_mx(
                    out=acc[:],
                    lhsT=w_codes[:, m_cols].bitcast(FP8X4),
                    lhsT_scale=w_plane[:, m_cols],
                    rhs=x_codes[:, n_cols].bitcast(FP8X4),
                    rhs_scale=x_plane[:, n_cols],
                    start=True,
                    stop=True,
                )
                nc.scalar.copy(y[t][:, a * BANK : (a + 1) * BANK], acc[:])

        d_words_picked = keep.tile([P, H], U32, name="d_words_picked", align_bytes=64)
        nc.vector.tensor_copy(d_words_picked[:], d_word_table[:].indirect(k1_sb[:]))
        for q in range(0, P, 32):
            nc.sync.dma_start(d_plane[q : q + 4, :].bitcast(I32), d_bytes_picked[q : q + 32 : 8, :].bitcast(I32))

        ident = keep.tile([P, P], F32, name="ident")
        make_identity(nc, ident[:])

        HV = V // 2

        def line_up(a, lined, z_grouped, groups):
            for tiles in groups:
                for t in tiles:
                    nc.vector.tensor_copy(lined[:, t, :], y[t][:].indirect(n1_sb[:, a * 32 : (a + 1) * 32]))
                pairs = lined[:, tiles.start : tiles.stop, :].rearrange("p i (v two) -> p (i v) two", two=2)
                pooled = keep.tile([P, len(tiles) * HV], F32, name=f"pooled{a}{tiles.start}")
                nc.vector.tensor_tensor(pooled[:], pairs[:, :, 0], pairs[:, :, 1], ALU.max)
                for i, t in enumerate(tiles):
                    nc.scalar.activation(
                        z_grouped[:, :, t], pooled[:, i * HV : (i + 1) * HV], COPY, scale=gs_sb[:, t : t + 1]
                    )

        old_first = keep.tile([P, V], F32, name="old_first")
        nc.vector.tensor_scalar(old_first[:], page[0][:].indirect(n2_sb[:]), 0.5, 0.0, ALU.mult, ALU.add)

        def fetch_old(a, rest):
            for t in range(1, PACK):
                nc.vector.tensor_scalar(
                    rest[:, t - 1, :], page[t][:].indirect(n2_sb[:, a * 16 : (a + 1) * 16]), 0.5, 0.0, ALU.mult, ALU.add
                )
            return [old_first[:, a * HV : (a + 1) * HV]] + [rest[:, i, :] for i in range(PACK - 1)]

        def quantise(a, z_grouped):
            z_codes = keep.tile([P, HV], U32, name=f"z_codes{a}", align_bytes=64)
            z_plane = keep.tile([P, HV], U8, name=f"z_plane{a}", align_bytes=64)
            nc.vector.quantize_mx(
                out=z_codes[:].bitcast(FP8X4), scales=z_plane[:], in_=z_grouped[:].rearrange("p v t -> p (v t)")
            )
            return z_codes, z_plane

        def turn_old(a, old, tags):
            old_t = []
            for u in range(2):
                acc = psum.tile([P, 2, 2, P], F32, name="acc")
                for i in range(2):
                    for b in range(2):
                        nc.tensor.transpose(acc[:, i, b, :], old[2 * u + i][:, b * P : (b + 1) * P], ident[:])
                turned = keep.tile([P, 2, 2, P], F32, name=f"old_t{a}{u}", tag=tags[u], align_bytes=64)
                nc.scalar.copy(turned[:], acc[:])
                old_t.append(turned)
            return old_t

        def second_product(a, z_codes, z_plane):
            neg_h_t = []
            for b in range(2):
                cols = slice(b * P, (b + 1) * P)
                acc = psum.tile([P, BANK], F32, name="acc")
                nc.tensor.matmul_mx(
                    out=acc[:],
                    lhsT=z_codes[:, cols].bitcast(FP8X4),
                    lhsT_scale=z_plane[:, cols],
                    rhs=d_words_picked[:].bitcast(FP8X4),
                    rhs_scale=d_plane[:],
                    start=True,
                    stop=True,
                )
                dealt = keep.tile([P, PACK, P], F32, name=f"neg_h_t{a}{b}")
                nc.scalar.activation(dealt[:], acc[:].rearrange("p (m t) -> p t m", t=PACK), COPY, scale=-0.0625)
                neg_h_t.append(dealt)
            return neg_h_t

        def turn_back(u, neg_h_t, old_t):
            neg_h = psum.tile([P, 2, HV], F32, name="acc")
            gap = psum.tile([P, 2, HV], F32, name="acc")
            for i in range(2):
                for b in range(2):
                    nc.tensor.transpose(neg_h[:, i, b * P : (b + 1) * P], neg_h_t[b][:, 2 * u + i, :], ident[:])
            for i in range(2):
                for b in range(2):
                    cols = slice(b * P, (b + 1) * P)
                    nc.tensor.matmul(
                        gap[:, i, cols], old_t[u][:, i, b, :], ident[:], start=True, stop=False, is_transpose=True
                    )
                    nc.tensor.matmul(
                        gap[:, i, cols], neg_h_t[b][:, 2 * u + i, :], ident[:], start=False, stop=True, is_transpose=True
                    )
            return neg_h, gap

        def leave_banks(a, u, banks):
            neg_h, gap = banks
            h = keep.tile([P, 2, HV], F32, name=f"h{a}{u}")
            nc.scalar.activation(h[:], neg_h[:], COPY, scale=-1.0)
            lift = keep.tile([P, 2, HV], F32, name=f"lift{a}{u}")
            nc.scalar.activation(lift[:], gap[:], RELU)
            return [(h[:, i, :], lift[:, i, :]) for i in range(2)]

        def scatter(a, t, terms):
            nc.vector.tensor_tensor(page[t][:].indirect(n2_sb[:, a * 16 : (a + 1) * 16]), *terms, ALU.add)

        z0 = keep.tile([P, HV, PACK], BF16, name="z0", align_bytes=64, tag="slot_g")
        lined0 = keep.tile([P, PACK, 2 * HV], F32, name="lined0", tag="slot_l0")
        line_up(0, lined0, z0, (range(0, 2), range(2, 4)))
        rest0 = keep.tile([P, PACK - 1, HV], F32, name="rest0", tag="slot_l0")
        old0 = fetch_old(0, rest0)
        q0 = quantise(0, z0)
        old_t0 = turn_old(0, old0, ("slot_z", "slot_o1"))
        neg_h_t0 = second_product(0, *q0)
        banks0 = [turn_back(u, neg_h_t0, old_t0) for u in range(2)]
        terms0 = leave_banks(0, 0, banks0[0])
        z1 = keep.tile([P, HV, PACK], BF16, name="z1", align_bytes=64, tag="slot_z")
        lined1 = keep.tile([P, PACK, 2 * HV], F32, name="lined1", align_bytes=64, tag="slot_g")
        line_up(1, lined1, z1, (range(0, 2), range(2, 3), range(3, 4)))
        scatter(0, 0, terms0[0])
        terms0 = terms0 + leave_banks(0, 1, banks0[1])
        q1 = quantise(1, z1)
        rest1 = keep.tile([P, PACK - 1, HV], F32, name="rest1", align_bytes=64, tag="slot_z")
        old1 = fetch_old(1, rest1)
        neg_h_t1 = second_product(1, *q1)
        for t in range(1, PACK):
            scatter(0, t, terms0[t])
        old_t1 = turn_old(1, old1, ("slot_o2", "slot_o3"))
        for u in range(2):
            terms = leave_banks(1, u, turn_back(u, neg_h_t1, old_t1))
            for i in range(2):
                scatter(1, 2 * u + i, terms[i])
                nc.sync.dma_start(out_rows[:, 2 * u + i, :], page[2 * u + i][:])
